import numpy as np
import ml_dtypes


def mxq(x, axis, fmt="e4m3"):
    dtype, down = {"e4m3": (ml_dtypes.float8_e4m3fn, 7), "e5m2": (ml_dtypes.float8_e5m2, 14)}[fmt]
    v = np.moveaxis(np.asarray(x, np.float32).astype(ml_dtypes.bfloat16).astype(np.float64), axis, -1)
    blocks = v.reshape(v.shape[:-1] + (-1, 32))
    amax = np.abs(blocks).max(-1, keepdims=True)
    byte = np.maximum(np.where(amax > 0, np.frexp(amax)[1] - 1 + 127, 0) - down, 1)
    scale = np.exp2(byte - 127.0)
    codes = (blocks / scale).astype(np.float32).astype(dtype).astype(np.float64)
    return np.moveaxis((codes * scale).reshape(v.shape), -1, axis)


WIDE = False


def mx_kscale(k):
    if not WIDE:
        return np.ones(k)
    levels = np.array([30, -30])
    if k % 512:
        return np.exp2(np.random.permutation(np.resize(levels, k // 32))).repeat(32)
    a = np.empty((k // 512, 16))
    for p in range(k // 512):
        a[p, :8] = np.random.permutation(np.resize(levels, 8))
        for g in range(8):
            far = levels[np.abs(levels - a[p, g]) >= 10]
            a[p, g + 8] = far[np.random.randint(len(far))]
    return np.exp2(a.ravel()).repeat(32)


def f64(x):
    return np.asarray(x).astype(np.float64)


K, L, M, T = 1024, 1024, 512, 1536


def setup_inputs():
    n = np.random.standard_normal
    s1 = mx_kscale(K)[:, None]
    s2 = mx_kscale(L)[:, None]
    m = np.exp(0.5 * n((1, T)))
    return {
        "w": (n((K, M)) / np.sqrt(K) / s1).astype(np.float32),
        "dy": (m * n((K, T)) * s1).astype(np.float32),
        "v": (n((L, M)) / np.sqrt(L) / s2).astype(np.float32),
        "e": (n((L, T)) * s2).astype(np.float32),
    }


def reference(w, dy, v, e):
    w_ = mxq(f64(w), 0, "e4m3")
    dy_ = mxq(f64(dy), 0, "e5m2")
    v_ = mxq(f64(v), 0, "e4m3")
    e_ = mxq(f64(e), 0, "e4m3")
    y = w_.T @ dy_ + v_.T @ e_
    return y

@@ -1,0 +1,139 @@
+from contextlib import ExitStack
+
+import concourse.mybir as mybir
+
+K, L, M, T = 1024, 1024, 512, 1536
+FLOPS = 2 * (K + L) * M * T
+
+F32 = mybir.dt.float32
+BF16 = mybir.dt.bfloat16
+U32 = mybir.dt.uint32
+U8 = mybir.dt.uint8
+E4M3 = mybir.dt.float8_e4m3fn_x4
+E5M2 = mybir.dt.float8_e5m2_x4
+
+P = 128
+J = 4
+K_PASS = P * J
+CHUNK = 512
+HALF = 256
+V_COLS = 128
+
+
+def tile_mix_aux_fm_none_kernel(tc, w, dy, v, e, out):
+    nc = tc.nc
+    hbm = {"w": w, "dy": dy, "v": v, "e": e}
+    fmt = {"w": E4M3, "dy": E5M2, "v": E4M3, "e": E4M3}
+    loads = [
+        ("w", 0, 0, 512),
+        ("dy", 0, 0, 1536),
+        ("w", 1, 0, 512),
+        ("dy", 1, 0, 1536),
+        ("v", 0, 0, 512),
+        ("v", 1, 0, 512),
+        ("e", 0, 0, 512),
+        ("e", 1, 0, 512),
+        ("e", 0, 512, 512),
+        ("e", 1, 512, 512),
+        ("e", 0, 1024, 512),
+        ("e", 1, 1024, 512),
+    ]
+
+    with ExitStack() as ctx:
+        keep = ctx.enter_context(tc.tile_pool(name="keep", bufs=1))
+        stage = ctx.enter_context(tc.tile_pool(name="stage", bufs=6))
+        psum = ctx.enter_context(tc.psum_pool(name="psum", bufs=2))
+        ctx.enter_context(tc.manual_schedule())
+
+        raw = {}
+        for name, g, c0, cols in loads:
+            t = keep.tile([P, J, cols], F32, name="raw_%s%d_%d" % (name, g, c0))
+            nc.sync.dma_start(
+                out=t[:],
+                in_=hbm[name][g * K_PASS : (g + 1) * K_PASS, c0 : c0 + cols].rearrange("(p j) c -> p j c", j=J),
+            )
+            for q in range(0, cols, CHUNK):
+                raw[name, g, (c0 + q) // CHUNK] = (t, q)
+
+        codes, scales = {}, {}
+        for name in ("w", "dy", "v", "e"):
+            width = hbm[name].shape[1]
+            codes[name] = keep.tile([P, 2, width], U32, name="codes_" + name, align_bytes=64)
+            scales[name] = keep.tile([P, 2, width], U8, name="scales_" + name, align_bytes=64)
+
+        def prep(name, g, c):
+            t, q = raw[name, g, c]
+            groups = []
+            for h in (0, HALF):
+                b = stage.tile([P, HALF, J], BF16, name="grouped", align_bytes=64)
+                for eng, lo, hi in ((nc.vector.tensor_copy, 0, V_COLS), (nc.scalar.copy, V_COLS, HALF)):
+                    eng(
+                        out=b[:, lo:hi, :].rearrange("p (c i) j -> p c j i", i=4),
+                        in_=t[:, :, q + h + lo : q + h + hi].rearrange("p j (c i) -> p c j i", i=4),
+                    )
+                groups.append(b)
+            for h, b in zip((0, HALF), groups):
+                cols = slice(c * CHUNK + h, c * CHUNK + h + HALF)
+                nc.vector.quantize_mx(
+                    out=codes[name][:, g, cols].bitcast(fmt[name]),
+                    scales=scales[name][:, g, cols],
+                    in_=b[:].rearrange("p c j -> p (c j)"),
+                )
+
+        acc = {}
+
+        def passes(c, sta, mov, g, start=False, stop=False):
+            for m in range(M // P):
+                if start:
+                    acc[c, m] = psum.tile([P, CHUNK], F32, name="acc%d" % m)
+                rows = slice(m * P, (m + 1) * P)
+                cols = slice(c * CHUNK, (c + 1) * CHUNK)
+                nc.tensor.matmul_mx(
+                    out=acc[c, m][:],
+                    lhsT=codes[sta][:, g, rows].bitcast(fmt[sta]),
+                    lhsT_scale=scales[sta][:, g, rows],
+                    rhs=codes[mov][:, g, cols].bitcast(fmt[mov]),
+                    rhs_scale=scales[mov][:, g, cols],
+                    start=start,
+                    stop=stop,
+                )
+
+        res = {(c, m): keep.tile([P, CHUNK], F32, name="res%d_%d" % (c, m)) for c in range(3) for m in range(M // P)}
+
+        def drain(c):
+            for m in range(M // P):
+                copy = nc.vector.tensor_copy if m % 2 else nc.scalar.copy
+                copy(out=res[c, m][:], in_=acc[c, m][:])
+                nc.sync.dma_start(out=out[m * P : (m + 1) * P, c * CHUNK : (c + 1) * CHUNK], in_=res[c, m][:])
+
+        prep("w", 0, 0)
+        prep("dy", 0, 0)
+        prep("dy", 0, 1)
+        prep("dy", 0, 2)
+        passes(0, "w", "dy", 0, start=True)
+        passes(1, "w", "dy", 0, start=True)
+        prep("w", 1, 0)
+        prep("dy", 1, 0)
+        prep("dy", 1, 1)
+        prep("dy", 1, 2)
+        passes(0, "w", "dy", 1)
+        passes(1, "w", "dy", 1)
+        prep("v", 0, 0)
+        prep("v", 1, 0)
+        prep("e", 0, 0)
+        passes(0, "v", "e", 0)
+        prep("e", 1, 0)
+        passes(0, "v", "e", 1, stop=True)
+        prep("e", 0, 1)
+        passes(1, "v", "e", 0)
+        drain(0)
+        passes(2, "w", "dy", 0, start=True)
+        passes(2, "w", "dy", 1)
+        prep("e", 1, 1)
+        passes(1, "v", "e", 1, stop=True)
+        prep("e", 0, 2)
+        passes(2, "v", "e", 0)
+        drain(1)
+        prep("e", 1, 2)
+        passes(2, "v", "e", 1, stop=True)
+        drain(2)

@@ -17,7 +17,7 @@ J = 4
 K_PASS = P * J
 CHUNK = 512
 HALF = 256
-V_COLS = 128
+V_COLS = 144
 
 
 def tile_mix_aux_fm_none_kernel(tc, w, dy, v, e, out):
@@ -28,13 +28,14 @@ def tile_mix_aux_fm_none_kernel(tc, w, dy, v, e, out):
         ("w", 0, 0, 512),
         ("dy", 0, 0, 1536),
         ("w", 1, 0, 512),
-        ("dy", 1, 0, 1536),
+        ("dy", 1, 0, 1024),
         ("v", 0, 0, 512),
         ("v", 1, 0, 512),
         ("e", 0, 0, 512),
         ("e", 1, 0, 512),
         ("e", 0, 512, 512),
         ("e", 1, 512, 512),
+        ("dy", 1, 1024, 512),
         ("e", 0, 1024, 512),
         ("e", 1, 1024, 512),
     ]
@@ -52,8 +53,7 @@ def tile_mix_aux_fm_none_kernel(tc, w, dy, v, e, out):
                 out=t[:],
                 in_=hbm[name][g * K_PASS : (g + 1) * K_PASS, c0 : c0 + cols].rearrange("(p j) c -> p j c", j=J),
             )
-            for q in range(0, cols, CHUNK):
-                raw[name, g, (c0 + q) // CHUNK] = (t, q)
+            raw[name, g, c0] = t
 
         codes, scales = {}, {}
         for name in ("w", "dy", "v", "e"):
@@ -61,35 +61,43 @@ def tile_mix_aux_fm_none_kernel(tc, w, dy, v, e, out):
             codes[name] = keep.tile([P, 2, width], U32, name="codes_" + name, align_bytes=64)
             scales[name] = keep.tile([P, 2, width], U8, name="scales_" + name, align_bytes=64)
 
-        def prep(name, g, c):
-            t, q = raw[name, g, c]
-            groups = []
-            for h in (0, HALF):
-                b = stage.tile([P, HALF, J], BF16, name="grouped", align_bytes=64)
-                for eng, lo, hi in ((nc.vector.tensor_copy, 0, V_COLS), (nc.scalar.copy, V_COLS, HALF)):
-                    eng(
-                        out=b[:, lo:hi, :].rearrange("p (c i) j -> p c j i", i=4),
-                        in_=t[:, :, q + h + lo : q + h + hi].rearrange("p j (c i) -> p c j i", i=4),
-                    )
-                groups.append(b)
-            for h, b in zip((0, HALF), groups):
-                cols = slice(c * CHUNK + h, c * CHUNK + h + HALF)
-                nc.vector.quantize_mx(
-                    out=codes[name][:, g, cols].bitcast(fmt[name]),
-                    scales=scales[name][:, g, cols],
-                    in_=b[:].rearrange("p c j -> p (c j)"),
+        def interleave(name, g, c0, h, v_cols):
+            b = stage.tile([P, HALF, J], BF16, name="grouped", align_bytes=64)
+            for copy, lo, hi in ((nc.vector.tensor_copy, 0, v_cols), (nc.scalar.copy, v_cols, HALF)):
+                copy(
+                    out=b[:, lo:hi, :].rearrange("p (c i) j -> p c j i", i=4),
+                    in_=raw[name, g, c0][:, :, h + lo : h + hi].rearrange("p j (c i) -> p c j i", i=4),
                 )
+            return b
+
+        def quantise(name, g, c0, h, b):
+            cols = slice(c0 + h, c0 + h + HALF)
+            nc.vector.quantize_mx(
+                out=codes[name][:, g, cols].bitcast(fmt[name]),
+                scales=scales[name][:, g, cols],
+                in_=b[:].rearrange("p c j -> p (c j)"),
+            )
+
+        def prep(name, g, c0, v_cols=V_COLS):
+            width = raw[name, g, c0].shape[2]
+            last = None
+            for h in range(0, width, HALF):
+                b = interleave(name, g, c0, h, v_cols)
+                if last is not None:
+                    quantise(name, g, c0, h - HALF, last)
+                last = b
+            quantise(name, g, c0, width - HALF, last)
 
         acc = {}
 
-        def passes(c, sta, mov, g, start=False, stop=False):
+        def passes(c, sta, mov, g, start=False, stop=False, n0=0, n=CHUNK):
             for m in range(M // P):
                 if start:
                     acc[c, m] = psum.tile([P, CHUNK], F32, name="acc%d" % m)
                 rows = slice(m * P, (m + 1) * P)
-                cols = slice(c * CHUNK, (c + 1) * CHUNK)
+                cols = slice(c * CHUNK + n0, c * CHUNK + n0 + n)
                 nc.tensor.matmul_mx(
-                    out=acc[c, m][:],
+                    out=acc[c, m][:, n0 : n0 + n],
                     lhsT=codes[sta][:, g, rows].bitcast(fmt[sta]),
                     lhsT_scale=scales[sta][:, g, rows],
                     rhs=codes[mov][:, g, cols].bitcast(fmt[mov]),
@@ -108,14 +116,10 @@ def tile_mix_aux_fm_none_kernel(tc, w, dy, v, e, out):
 
         prep("w", 0, 0)
         prep("dy", 0, 0)
-        prep("dy", 0, 1)
-        prep("dy", 0, 2)
         passes(0, "w", "dy", 0, start=True)
         passes(1, "w", "dy", 0, start=True)
         prep("w", 1, 0)
         prep("dy", 1, 0)
-        prep("dy", 1, 1)
-        prep("dy", 1, 2)
         passes(0, "w", "dy", 1)
         passes(1, "w", "dy", 1)
         prep("v", 0, 0)
@@ -124,16 +128,18 @@ def tile_mix_aux_fm_none_kernel(tc, w, dy, v, e, out):
         passes(0, "v", "e", 0)
         prep("e", 1, 0)
         passes(0, "v", "e", 1, stop=True)
-        prep("e", 0, 1)
+        prep("e", 0, 512)
         passes(1, "v", "e", 0)
         drain(0)
         passes(2, "w", "dy", 0, start=True)
-        passes(2, "w", "dy", 1)
-        prep("e", 1, 1)
+        prep("e", 1, 512)
         passes(1, "v", "e", 1, stop=True)
-        prep("e", 0, 2)
-        passes(2, "v", "e", 0)
+        prep("dy", 1, 1024)
+        passes(2, "w", "dy", 1)
         drain(1)
-        prep("e", 1, 2)
-        passes(2, "v", "e", 1, stop=True)
+        prep("e", 0, 1024)
+        passes(2, "v", "e", 0)
+        prep("e", 1, 1024, 168)
+        passes(2, "v", "e", 1, n0=0, n=HALF)
+        passes(2, "v", "e", 1, stop=True, n0=HALF, n=HALF)
         drain(2)

@@ -27,17 +27,16 @@ def tile_mix_aux_fm_none_kernel(tc, w, dy, v, e, out):
     loads = [
         ("w", 0, 0, 512),
         ("dy", 0, 0, 1536),
-        ("w", 1, 0, 512),
-        ("dy", 1, 0, 1024),
+        ("e", 0, 0, 1024),
         ("v", 0, 0, 512),
+        ("e", 1, 0, 1024),
         ("v", 1, 0, 512),
-        ("e", 0, 0, 512),
-        ("e", 1, 0, 512),
-        ("e", 0, 512, 512),
-        ("e", 1, 512, 512),
-        ("dy", 1, 1024, 512),
-        ("e", 0, 1024, 512),
+        ("w", 1, 0, 512),
+        ("dy", 1, 512, 512),
+        ("dy", 1, 0, 512),
         ("e", 1, 1024, 512),
+        ("e", 0, 1024, 512),
+        ("dy", 1, 1024, 512),
     ]
 
     with ExitStack() as ctx:
@@ -106,40 +105,46 @@ def tile_mix_aux_fm_none_kernel(tc, w, dy, v, e, out):
                     stop=stop,
                 )
 
-        res = {(c, m): keep.tile([P, CHUNK], F32, name="res%d_%d" % (c, m)) for c in range(3) for m in range(M // P)}
+        res = [keep.tile([P, M // P, CHUNK], F32, name="res%d" % c) for c in range(3)]
 
         def drain(c):
             for m in range(M // P):
                 copy = nc.vector.tensor_copy if m % 2 else nc.scalar.copy
-                copy(out=res[c, m][:], in_=acc[c, m][:])
-                nc.sync.dma_start(out=out[m * P : (m + 1) * P, c * CHUNK : (c + 1) * CHUNK], in_=res[c, m][:])
+                copy(out=res[c][:, m, :], in_=acc[c, m][:])
+
+        def store(c, m0, m1):
+            rows = out[m0 * P : m1 * P, c * CHUNK : (c + 1) * CHUNK]
+            nc.sync.dma_start(out=rows.rearrange("(m p) t -> p m t", p=P), in_=res[c][:, m0:m1, :])
 
         prep("w", 0, 0)
         prep("dy", 0, 0)
         passes(0, "w", "dy", 0, start=True)
         passes(1, "w", "dy", 0, start=True)
-        prep("w", 1, 0)
-        prep("dy", 1, 0)
-        passes(0, "w", "dy", 1)
-        passes(1, "w", "dy", 1)
-        prep("v", 0, 0)
-        prep("v", 1, 0)
         prep("e", 0, 0)
+        prep("v", 0, 0)
         passes(0, "v", "e", 0)
-        prep("e", 1, 0)
-        passes(0, "v", "e", 1, stop=True)
-        prep("e", 0, 512)
         passes(1, "v", "e", 0)
-        drain(0)
-        passes(2, "w", "dy", 0, start=True)
-        prep("e", 1, 512)
-        passes(1, "v", "e", 1, stop=True)
-        prep("dy", 1, 1024)
-        passes(2, "w", "dy", 1)
+        prep("e", 1, 0)
+        prep("v", 1, 0)
+        passes(0, "v", "e", 1)
+        passes(1, "v", "e", 1)
+        prep("w", 1, 0)
+        prep("dy", 1, 512)
+        passes(1, "w", "dy", 1, stop=True)
+        prep("dy", 1, 0)
+        passes(0, "w", "dy", 1, stop=True)
         drain(1)
+        store(1, 0, 4)
+        passes(2, "w", "dy", 0, start=True)
+        prep("e", 1, 1024)
+        passes(2, "v", "e", 1)
+        drain(0)
+        store(0, 0, 4)
         prep("e", 0, 1024)
         passes(2, "v", "e", 0)
-        prep("e", 1, 1024, 168)
-        passes(2, "v", "e", 1, n0=0, n=HALF)
-        passes(2, "v", "e", 1, stop=True, n0=HALF, n=HALF)
+        prep("dy", 1, 1024, 168)
+        passes(2, "w", "dy", 1, stop=True)
         drain(2)
+        store(2, 0, 1)
+        store(2, 1, 2)
+        store(2, 2, 4)

from contextlib import ExitStack

import concourse.mybir as mybir

K, L, M, T = 1024, 1024, 512, 1536
FLOPS = 2 * (K + L) * M * T

F32 = mybir.dt.float32
BF16 = mybir.dt.bfloat16
U32 = mybir.dt.uint32
U8 = mybir.dt.uint8
E4M3 = mybir.dt.float8_e4m3fn_x4
E5M2 = mybir.dt.float8_e5m2_x4

P = 128
J = 4
K_PASS = P * J
CHUNK = 512
HALF = 256
V_COLS = 144


def tile_mix_aux_fm_none_kernel(tc, w, dy, v, e, out):
    nc = tc.nc
    hbm = {"w": w, "dy": dy, "v": v, "e": e}
    fmt = {"w": E4M3, "dy": E5M2, "v": E4M3, "e": E4M3}
    loads = [
        ("w", 0, 0, 512),
        ("dy", 0, 0, 1536),
        ("e", 0, 0, 1024),
        ("v", 0, 0, 512),
        ("e", 1, 0, 1024),
        ("v", 1, 0, 512),
        ("w", 1, 0, 512),
        ("dy", 1, 512, 512),
        ("dy", 1, 0, 512),
        ("e", 1, 1024, 512),
        ("e", 0, 1024, 512),
        ("dy", 1, 1024, 512),
    ]

    with ExitStack() as ctx:
        keep = ctx.enter_context(tc.tile_pool(name="keep", bufs=1))
        stage = ctx.enter_context(tc.tile_pool(name="stage", bufs=6))
        psum = ctx.enter_context(tc.psum_pool(name="psum", bufs=2))
        ctx.enter_context(tc.manual_schedule())

        raw = {}
        for name, g, c0, cols in loads:
            t = keep.tile([P, J, cols], F32, name="raw_%s%d_%d" % (name, g, c0))
            nc.sync.dma_start(
                out=t[:],
                in_=hbm[name][g * K_PASS : (g + 1) * K_PASS, c0 : c0 + cols].rearrange("(p j) c -> p j c", j=J),
            )
            raw[name, g, c0] = t

        codes, scales = {}, {}
        for name in ("w", "dy", "v", "e"):
            width = hbm[name].shape[1]
            codes[name] = keep.tile([P, 2, width], U32, name="codes_" + name, align_bytes=64)
            scales[name] = keep.tile([P, 2, width], U8, name="scales_" + name, align_bytes=64)

        def interleave(name, g, c0, h, v_cols):
            b = stage.tile([P, HALF, J], BF16, name="grouped", align_bytes=64)
            for copy, lo, hi in ((nc.vector.tensor_copy, 0, v_cols), (nc.scalar.copy, v_cols, HALF)):
                copy(
                    out=b[:, lo:hi, :].rearrange("p (c i) j -> p c j i", i=4),
                    in_=raw[name, g, c0][:, :, h + lo : h + hi].rearrange("p j (c i) -> p c j i", i=4),
                )
            return b

        def quantise(name, g, c0, h, b):
            cols = slice(c0 + h, c0 + h + HALF)
            nc.vector.quantize_mx(
                out=codes[name][:, g, cols].bitcast(fmt[name]),
                scales=scales[name][:, g, cols],
                in_=b[:].rearrange("p c j -> p (c j)"),
            )

        def prep(name, g, c0, v_cols=V_COLS):
            width = raw[name, g, c0].shape[2]
            last = None
            for h in range(0, width, HALF):
                b = interleave(name, g, c0, h, v_cols)
                if last is not None:
                    quantise(name, g, c0, h - HALF, last)
                last = b
            quantise(name, g, c0, width - HALF, last)

        acc = {}

        def passes(c, sta, mov, g, start=False, stop=False, n0=0, n=CHUNK):
            for m in range(M // P):
                if start:
                    acc[c, m] = psum.tile([P, CHUNK], F32, name="acc%d" % m)
                rows = slice(m * P, (m + 1) * P)
                cols = slice(c * CHUNK + n0, c * CHUNK + n0 + n)
                nc.tensor.matmul_mx(
                    out=acc[c, m][:, n0 : n0 + n],
                    lhsT=codes[sta][:, g, rows].bitcast(fmt[sta]),
                    lhsT_scale=scales[sta][:, g, rows],
                    rhs=codes[mov][:, g, cols].bitcast(fmt[mov]),
                    rhs_scale=scales[mov][:, g, cols],
                    start=start,
                    stop=stop,
                )

        res = [keep.tile([P, M // P, CHUNK], F32, name="res%d" % c) for c in range(3)]

        def drain(c):
            for m in range(M // P):
                copy = nc.vector.tensor_copy if m % 2 else nc.scalar.copy
                copy(out=res[c][:, m, :], in_=acc[c, m][:])

        def store(c, m0, m1):
            rows = out[m0 * P : m1 * P, c * CHUNK : (c + 1) * CHUNK]
            nc.sync.dma_start(out=rows.rearrange("(m p) t -> p m t", p=P), in_=res[c][:, m0:m1, :])

        prep("w", 0, 0)
        prep("dy", 0, 0)
        passes(0, "w", "dy", 0, start=True)
        passes(1, "w", "dy", 0, start=True)
        prep("e", 0, 0)
        prep("v", 0, 0)
        passes(0, "v", "e", 0)
        passes(1, "v", "e", 0)
        prep("e", 1, 0)
        prep("v", 1, 0)
        passes(0, "v", "e", 1)
        passes(1, "v", "e", 1)
        prep("w", 1, 0)
        prep("dy", 1, 512)
        passes(1, "w", "dy", 1, stop=True)
        prep("dy", 1, 0)
        passes(0, "w", "dy", 1, stop=True)
        drain(1)
        store(1, 0, 4)
        passes(2, "w", "dy", 0, start=True)
        prep("e", 1, 1024)
        passes(2, "v", "e", 1)
        drain(0)
        store(0, 0, 4)
        prep("e", 0, 1024)
        passes(2, "v", "e", 0)
        prep("dy", 1, 1024, 168)
        passes(2, "w", "dy", 1, stop=True)
        drain(2)
        store(2, 0, 1)
        store(2, 1, 2)
        store(2, 2, 4)
